import numpy as np
import ml_dtypes


def mxq(x, axis, fmt="e4m3"):
    dtype, down = {"e4m3": (ml_dtypes.float8_e4m3fn, 7), "e5m2": (ml_dtypes.float8_e5m2, 14)}[fmt]
    v = np.moveaxis(np.asarray(x, np.float32).astype(ml_dtypes.bfloat16).astype(np.float64), axis, -1)
    blocks = v.reshape(v.shape[:-1] + (-1, 32))
    amax = np.abs(blocks).max(-1, keepdims=True)
    byte = np.maximum(np.where(amax > 0, np.frexp(amax)[1] - 1 + 127, 0) - down, 1)
    scale = np.exp2(byte - 127.0)
    codes = (blocks / scale).astype(np.float32).astype(dtype).astype(np.float64)
    return np.moveaxis((codes * scale).reshape(v.shape), -1, axis)


WIDE = False


def mx_kscale(k):
    if not WIDE:
        return np.ones(k)
    levels = np.array([10, -10, 5, -5, 0])
    if k % 512:
        return np.exp2(np.random.permutation(np.resize(levels, k // 32))).repeat(32)
    a = np.empty((k // 512, 16))
    for p in range(k // 512):
        a[p, :8] = np.random.permutation(np.resize(levels, 8))
        for g in range(8):
            far = levels[np.abs(levels - a[p, g]) >= 10]
            a[p, g + 8] = far[np.random.randint(len(far))]
    return np.exp2(a.ravel()).repeat(32)


def f64(x):
    return np.asarray(x).astype(np.float64)


def striped(idx):
    return np.tile(idx.reshape(-1, 16).T, (8, 1)).astype(np.uint16)


def unstriped(offs):
    return offs[:16].T.reshape(-1).astype(np.int64)


E2M1 = np.array([0.0, 0.5, 1.0, 1.5, 2.0, 3.0, 4.0, 6.0, -0.0, -0.5, -1.0, -1.5, -2.0, -3.0, -4.0, -6.0])


def pack_weight(w, fmt):
    k, n = w.shape
    w = f64(np.asarray(w, np.float32).astype(ml_dtypes.bfloat16)).reshape(k // 32, 32, n)
    amax = np.abs(w).max(1)
    if fmt == "e4m3":
        byte = np.frexp(amax)[1] - 1 + 127 - 7
    else:
        mant, ex = np.frexp(amax / 6.0)
        byte = np.where(mant > 0.5, ex, ex - 1) + 127
    byte = np.clip(np.where(amax > 0, byte, 1), 1, 254)
    scaled = (w * np.exp2(127.0 - byte)[:, None, :]).reshape(k, n).astype(np.float32)
    by_word = np.ascontiguousarray(scaled.reshape(k // 512, 128, 4, n).transpose(0, 1, 3, 2))
    if fmt == "e4m3":
        words = by_word.astype(ml_dtypes.float8_e4m3fn).view(np.uint8)
    else:
        c = by_word.astype(ml_dtypes.float4_e2m1fn).view(np.uint8) & 0xF
        words = (c[..., 0::2] | (c[..., 1::2] << 4)).reshape(k // 512, 128, 2 * n)
    return np.ascontiguousarray(words), np.ascontiguousarray(byte.astype(np.uint8).reshape(k // 512, 16, n))


def unpack_weight(words, scales, fmt):
    g, _, n = scales.shape
    words = np.ascontiguousarray(words).reshape(g, 128, n, -1)
    if fmt == "e4m3":
        vals = words.view(ml_dtypes.float8_e4m3fn).astype(np.float64)
    else:
        nib = np.empty((g, 128, n, 4), np.uint8)
        nib[..., 0::2] = words & 0xF
        nib[..., 1::2] = words >> 4
        vals = E2M1[nib]
    vals = vals * np.repeat(np.exp2(scales.astype(np.float64) - 127.0), 8, axis=1)[..., None]
    return vals.transpose(0, 1, 3, 2).reshape(g * 512, n)


def gelu(v):
    return 0.5 * v * (1.0 + np.tanh(np.sqrt(2.0 / np.pi) * (v + 0.044715 * v**3)))


K, T, S, P, H, N = 1024, 2048, 1024, 512, 512, 768

def setup_inputs():
    n = np.random.standard_normal
    s, u = mx_kscale(K)[:, None], mx_kscale(H)[:, None]
    tab_words, tab_scales = pack_weight(n((K, T)) * s, "e4m3")
    w2_words, w2_scales = pack_weight(0.75 * n((K, H)) / np.sqrt(K) / s, "e2m1")
    w3_words, w3_scales = pack_weight(0.4 * n((K, H)) / np.sqrt(K) / s, "e4m3")
    w5_words, w5_scales = pack_weight(n((H, N)) / np.sqrt(H) / u, "e2m1")
    return {
        "tab_words": tab_words, "tab_scales": tab_scales,
        "offs": striped(np.random.permutation(T)[:S]),
        "pos1": striped(np.random.permutation(S)[:P]),
        "pos2": striped(np.random.permutation(S)[:P]),
        "w1": (0.75 * n((K, H)) / np.sqrt(K) / s).astype(np.float32),
        "w2_words": w2_words, "w2_scales": w2_scales,
        "w3_words": w3_words, "w3_scales": w3_scales,
        "temp": np.random.uniform(0.4, 1.6, H).astype(np.float32),
        "thr": n(H).astype(np.float32),
        "lean": (0.4 * n(H) - 0.3).astype(np.float32),
        "chair": (1.8 * n((H, P)) * u).astype(np.float32),
        "w4": (1.3 * n((H, N)) / np.sqrt(H) / u).astype(np.float32),
        "w5_words": w5_words, "w5_scales": w5_scales,
    }

def reference(tab_words, tab_scales, offs, pos1, pos2, w1, w2_words, w2_scales, w3_words, w3_scales,
              temp, thr, lean, chair, w4, w5_words, w5_scales):
    v = unpack_weight(tab_words, tab_scales, "e4m3")[:, unstriped(offs)]
    W1 = mxq(f64(w1), 0, "e4m3")
    W2 = unpack_weight(w2_words, w2_scales, "e2m1")
    W3 = unpack_weight(w3_words, w3_scales, "e4m3")
    h = np.maximum(W1.T @ v + W3.T @ v, W2.T @ v + W3.T @ v)
    top = h.max(axis=1)
    a = np.exp(f64(temp)[:, None] * (h[:, unstriped(pos1)] - top[:, None]))
    c = 1.0 / (1.0 + np.exp(-(h[:, unstriped(pos2)] + f64(thr)[:, None])))
    m = mxq(np.maximum(a, c + f64(lean)[:, None]) * f64(chair), 0, "e4m3")
    W4 = mxq(f64(w4), 0, "e4m3")
    W5 = unpack_weight(w5_words, w5_scales, "e2m1")
    y = W4.T @ m
    z = W5.T @ m
    return y - np.square(z)

@@ -1,0 +1,290 @@
+from contextlib import ExitStack
+
+import concourse.mybir as mybir
+
+K, T, S, M, H, N = 1024, 2048, 1024, 512, 512, 768
+FLOPS = 2 * (4 * K * H * S + 2 * H * N * M)
+
+F32 = mybir.dt.float32
+BF16 = mybir.dt.bfloat16
+I32 = mybir.dt.int32
+U32 = mybir.dt.uint32
+U16 = mybir.dt.uint16
+U8 = mybir.dt.uint8
+FP8X4 = mybir.dt.float8_e4m3fn_x4
+FP4X4 = mybir.dt.float4_e2m1fn_x4
+ACT = mybir.ActivationFunctionType
+ALU = mybir.AluOpType
+AX = mybir.AxisListType
+
+P = 128
+PACK = 4
+PASSES = K // (P * PACK)
+BANK = 512
+QUADS = 4
+VECTOR_SHARE = 80
+
+
+def tile_list_sculpture_jury_scores_kernel(
+    tc, tab_words, tab_scales, offs, pos1, pos2, w1, w2_words, w2_scales, w3_words, w3_scales,
+    temp, thr, lean, chair, w4, w5_words, w5_scales, out,
+):
+    nc = tc.nc
+    with ExitStack() as ctx:
+        sb = ctx.enter_context(tc.tile_pool(name="sb", bufs=1))
+        psum = ctx.enter_context(tc.psum_pool(name="psum", bufs=4))
+
+        def sbuf(shape, dtype, name, tag=""):
+            return sb.tile(shape, dtype, name=name, tag=tag or name, align_bytes=64)
+
+        tab_sc = sbuf([P, T], U8, "tab_sc")
+        w3_sc_raw = sbuf([P, H], U8, "w3_sc_raw")
+        w2_sc_raw = sbuf([P, PASSES, H], U8, "w2_sc_raw")
+        v_sc1 = sbuf([P, S], U8, "v_sc1")
+        w5_sc = sbuf([P, N], U8, "w5_sc")
+        nc.gpsimd.memset(tab_sc[:].bitcast(I32), 0)
+        nc.vector.memset(w3_sc_raw[:].bitcast(I32), 0)
+        nc.vector.memset(w2_sc_raw[:].bitcast(I32), 0)
+        nc.gpsimd.memset(v_sc1[:].bitcast(I32), 0)
+        nc.gpsimd.memset(w5_sc[:].bitcast(I32), 0)
+
+        tab_w = [sbuf([P, T], U32, f"tab_w{a}") for a in range(PASSES)]
+        w3_raw = [sbuf([P, H], U32, f"w3_raw{a}") for a in range(PASSES)]
+        w2_raw = sbuf([P, PASSES, H], U16, "w2_raw")
+        w1_raw = [sbuf([P, PACK, H], F32, f"w1_raw{a}") for a in range(PASSES)]
+        idx = sbuf([P, S // 16], U16, "idx")
+        p1 = sbuf([P, M // 16], U16, "p1")
+        p2 = sbuf([P, M // 16], U16, "p2")
+        temp_c = sbuf([P, PACK], F32, "temp_c")
+        thr_c = sbuf([P, PACK], F32, "thr_c", tag="thr_then_edges")
+        lean_c = sbuf([P, PACK], F32, "lean_c")
+        chair_sb = sbuf([P, PACK, M], F32, "chair_sb")
+        w4_raw = sbuf([P, PACK, N], F32, "w4_raw")
+        w5_w = sbuf([P, N], U16, "w5_w")
+
+        def load_words(dst, src):
+            nc.sync.dma_start(out=dst[:].bitcast(I32), in_=src.rearrange("p c i -> p (c i)").bitcast(I32))
+
+        load_words(tab_w[0], tab_words[0])
+        nc.sync.dma_start(idx[:], offs)
+        for q in range(QUADS):
+            nc.sync.dma_start(out=tab_sc[32 * q : 32 * q + 8, :].bitcast(I32),
+                              in_=tab_scales[:, 4 * q : 4 * q + 4, :].bitcast(I32))
+        load_words(w3_raw[0], w3_words[0])
+        for q in range(QUADS):
+            nc.sync.dma_start(out=w3_sc_raw[32 * q : 32 * q + 8, :].bitcast(I32),
+                              in_=w3_scales[:, 4 * q : 4 * q + 4, :].bitcast(I32))
+        load_words(tab_w[1], tab_words[1])
+        for q in range(QUADS):
+            nc.sync.dma_start(out=w2_sc_raw[32 * q : 32 * q + 4, :, :].bitcast(I32),
+                              in_=w2_scales[:, 4 * q : 4 * q + 4, :].rearrange("a r c -> r a c").bitcast(I32))
+        nc.sync.dma_start(out=w2_raw[:].bitcast(I32), in_=w2_words.rearrange("a p c -> p a c").bitcast(I32))
+        load_words(w3_raw[1], w3_words[1])
+        for a in range(PASSES):
+            nc.sync.dma_start(out=w1_raw[a][:],
+                              in_=w1[a * 512 : (a + 1) * 512, :].rearrange("(p j) c -> p j c", j=PACK))
+        nc.sync.dma_start(p1[:], pos1)
+        nc.sync.dma_start(p2[:], pos2)
+        for dst, src in ((temp_c, temp), (thr_c, thr), (lean_c, lean)):
+            nc.sync.dma_start(out=dst[:], in_=src.rearrange("(p t) -> p t", t=PACK))
+        nc.sync.dma_start(out=w4_raw[:], in_=w4.rearrange("(p j) n -> p j n", j=PACK))
+        nc.sync.dma_start(out=chair_sb[:], in_=chair.rearrange("(p t) m -> p t m", t=PACK))
+        nc.sync.dma_start(out=w5_w[:].bitcast(I32), in_=w5_words[0].bitcast(I32))
+        for q in range(QUADS):
+            nc.sync.dma_start(out=w5_sc[32 * q : 32 * q + 4, :].bitcast(I32),
+                              in_=w5_scales[0, 4 * q : 4 * q + 4, :].bitcast(I32))
+
+        v_w = [sbuf([P, S], U32, f"v_w{a}") for a in range(PASSES)]
+        v_sc = sbuf([P, S], U8, "v_sc")
+        w3_w = [sbuf([P, H], U32, f"w3_w{a}") for a in range(PASSES)]
+        w2_w = sbuf([P, PASSES, H], U16, "w2_w")
+        w3_sc = sbuf([P, H], U8, "w3_sc")
+        w2_sc = sbuf([P, PASSES, H], U8, "w2_sc")
+
+        def cols(half):
+            return slice(half * BANK, (half + 1) * BANK)
+
+        def entries(half):
+            return idx[:, half * (BANK // 16) : (half + 1) * (BANK // 16)]
+
+        def dealt(ap):
+            return ap.rearrange("p (t m) -> p m t", t=PACK)
+
+        def natural(ap):
+            return ap.rearrange("p (m t) -> p m t", t=PACK)
+
+        nc.vector.tensor_copy(v_sc[:, cols(0)], tab_sc[:].indirect(entries(0)))
+        nc.vector.tensor_copy(v_w[0][:, cols(0)], tab_w[0][:].indirect(entries(0)))
+        nc.vector.tensor_copy(v_sc[:, cols(1)], tab_sc[:].indirect(entries(1)))
+        nc.vector.tensor_copy(v_w[0][:, cols(1)], tab_w[0][:].indirect(entries(1)))
+        for half in range(2):
+            nc.vector.tensor_copy(v_w[1][:, cols(half)], tab_w[1][:].indirect(entries(half)))
+        nc.scalar.copy(dealt(w3_w[0][:]), natural(w3_raw[0][:]))
+        nc.gpsimd.tensor_copy(w3_sc[:].rearrange("p (t m) -> p t m", t=PACK),
+                              w3_sc_raw[:].rearrange("p (m t) -> p t m", t=PACK))
+        for a in range(PASSES):
+            nc.gpsimd.tensor_copy(w2_sc[:, a, :].rearrange("p (t m) -> p t m", t=PACK),
+                                  w2_sc_raw[:, a, :].rearrange("p (m t) -> p t m", t=PACK))
+        for q in range(QUADS):
+            nc.scalar.dma_start(out=v_sc1[32 * q : 32 * q + 4, :].bitcast(I32),
+                                in_=v_sc[32 * q + 4 : 32 * q + 8, :].bitcast(I32))
+        nc.scalar.copy(dealt(w2_w[:, 0, :]), natural(w2_raw[:, 0, :]))
+        nc.scalar.copy(dealt(w3_w[1][:]), natural(w3_raw[1][:]))
+        nc.scalar.copy(dealt(w2_w[:, 1, :]), natural(w2_raw[:, 1, :]))
+
+        w1_w = [sbuf([P, H], U32, f"w1_w{a}") for a in range(PASSES)]
+        w1_sc = [sbuf([P, H], U8, f"w1_sc{a}") for a in range(PASSES)]
+        for a in range(PASSES):
+            w1_bf = sbuf([P, H * PACK], BF16, f"w1_bf{a}")
+            dst = w1_bf[:].rearrange("p (t m j) -> p m j t", t=PACK, j=PACK)
+            src = w1_raw[a][:].rearrange("p j (m t) -> p m j t", t=PACK)
+            nc.vector.tensor_copy(dst[:, :VECTOR_SHARE], src[:, :VECTOR_SHARE])
+            nc.scalar.activation(dst[:, VECTOR_SHARE:], src[:, VECTOR_SHARE:], ACT.Copy)
+            nc.vector.quantize_mx(out=w1_w[a][:].bitcast(FP8X4), scales=w1_sc[a][:], in_=w1_bf[:])
+
+        def rows(t):
+            return slice(t * P, (t + 1) * P)
+
+        def pass_w3(acc, t, half, a, start):
+            nc.tensor.matmul_mx(acc[:], lhsT=w3_w[a][:, rows(t)].bitcast(FP8X4), lhsT_scale=w3_sc[4 * a :, rows(t)],
+                                rhs=v_w[a][:, cols(half)].bitcast(FP8X4), rhs_scale=v_sc[4 * a :, cols(half)],
+                                start=start, stop=False)
+
+        def pass_w1(acc, t, half, a, stop):
+            nc.tensor.matmul_mx(acc[:], lhsT=w1_w[a][:, rows(t)].bitcast(FP8X4), lhsT_scale=w1_sc[a][:, rows(t)],
+                                rhs=v_w[a][:, cols(half)].bitcast(FP8X4), rhs_scale=v_sc[4 * a :, cols(half)],
+                                start=False, stop=stop)
+
+        def pass_w2(acc, t, half, a, stop):
+            plane = (v_sc, v_sc1)[a]
+            nc.tensor.matmul_mx(acc[:], lhsT=w2_w[:, a, rows(t)].bitcast(FP4X4), lhsT_scale=w2_sc[:, a, rows(t)],
+                                rhs=v_w[a][:, cols(half)].bitcast(FP8X4), rhs_scale=plane[:, cols(half)],
+                                start=False, stop=stop)
+
+        h = [sbuf([P, S], F32, f"h{t}") for t in range(PACK)]
+        top = sbuf([P, PACK], F32, "top")
+        bias01 = sbuf([P, 2], F32, "bias01", tag="bias_then_faces")
+        bias23 = sbuf([P, 2], F32, "bias23")
+
+        def bias_col(t):
+            return (bias01, bias23)[t // 2][:, t % 2 : t % 2 + 1]
+
+        def join(t, half, acc13, acc23):
+            other = sbuf([P, BANK], F32, f"sum23_{t}_{half}")
+            nc.scalar.activation(other[:], acc23[:], ACT.Copy)
+            nc.vector.tensor_tensor(h[t][:, cols(half)], acc13[:], other[:], ALU.max)
+
+        def row_max(t):
+            nc.vector.reduce_max(top[:, t : t + 1], h[t][:], AX.X)
+            nc.vector.tensor_scalar(bias_col(t), top[:, t : t + 1], temp_c[:, t : t + 1], -1.0, ALU.mult, ALU.mult)
+
+        acc13, acc23 = {}, {}
+        for half in range(2):
+            for t in range(2):
+                acc13[t, half] = psum.tile([P, BANK], F32, name="acc13", tag="first")
+                acc23[t, half] = psum.tile([P, BANK], F32, name="acc23", tag="second")
+                pass_w3(acc13[t, half], t, half, 0, True)
+                pass_w3(acc23[t, half], t, half, 0, True)
+        for half in range(2):
+            for t in range(2):
+                pass_w2(acc23[t, half], t, half, 0, False)
+        for half in range(2):
+            for t in range(2):
+                pass_w3(acc13[t, half], t, half, 1, False)
+                pass_w3(acc23[t, half], t, half, 1, False)
+        for t in range(2):
+            for half in range(2):
+                pass_w2(acc23[t, half], t, half, 1, True)
+        edges01 = sbuf([P, 2, M], F32, "edges01")
+        for t in range(2):
+            for half in range(2):
+                pass_w1(acc13[t, half], t, half, 0, False)
+            for half in range(2):
+                pass_w1(acc13[t, half], t, half, 1, True)
+                join(t, half, acc13[t, half], acc23[t, half])
+            row_max(t)
+            nc.scalar.activation(edges01[:, t, :], h[t][:].indirect(p1[:]), ACT.Exp,
+                                 bias=bias_col(t), scale=temp_c[:, t : t + 1])
+        for t in range(2, PACK):
+            for half in range(2):
+                b = psum.tile([P, BANK], F32, name="acc23", tag="second")
+                pass_w3(b, t, half, 0, True)
+                pass_w2(b, t, half, 0, False)
+                pass_w3(b, t, half, 1, False)
+                pass_w2(b, t, half, 1, True)
+                c = psum.tile([P, BANK], F32, name="acc13", tag="first")
+                pass_w3(c, t, half, 0, True)
+                pass_w3(c, t, half, 1, False)
+                pass_w1(c, t, half, 0, False)
+                pass_w1(c, t, half, 1, True)
+                join(t, half, c, b)
+            row_max(t)
+
+        HALF = M // 2
+        faces01 = sbuf([P, 2, M], F32, "faces01", tag="bias_then_faces")
+        faces23 = sbuf([P, 2, M], F32, "faces23")
+        for t in range(PACK):
+            nc.scalar.activation((faces01, faces23)[t // 2][:, t % 2, :], h[t][:].indirect(p2[:]), ACT.Sigmoid,
+                                 bias=thr_c[:, t : t + 1])
+        edges23 = sbuf([P, 2, M], F32, "edges23", tag="thr_then_edges")
+
+        m_bf = sbuf([P, M * PACK], BF16, "m_bf")
+        m_w = sbuf([P, M], U32, "m_w")
+        m_sc = sbuf([P, M], U8, "m_sc")
+        larger = sbuf([P, PACK, M], F32, "larger")
+
+        def weigh(pair, lo, hi):
+            dst = m_bf[:, lo * PACK : hi * PACK].rearrange("p (c i t) -> p c t i", i=4, t=PACK)
+            nc.vector.tensor_tensor(
+                dst[:, :, 2 * pair : 2 * pair + 2, :],
+                larger[:, 2 * pair : 2 * pair + 2, lo:hi].rearrange("p t (c i) -> p c t i", i=4),
+                chair_sb[:, 2 * pair : 2 * pair + 2, lo:hi].rearrange("p t (c i) -> p c t i", i=4),
+                ALU.mult)
+
+        for t in range(2):
+            nc.vector.scalar_tensor_tensor(larger[:, t, :], faces01[:, t, :], lean_c[:, t : t + 1], edges01[:, t, :],
+                                           ALU.add, ALU.max)
+        weigh(0, 0, M)
+
+        w4_bf = sbuf([P, N * PACK], BF16, "w4_bf")
+        w4_w = sbuf([P, N], U32, "w4_w")
+        w4_sc = sbuf([P, N], U8, "w4_sc")
+        for g in range(2):
+            lo, hi = g * N // 2, (g + 1) * N // 2
+            nc.gpsimd.tensor_scalar(
+                w4_bf[:, lo * PACK : hi * PACK].rearrange("p (n j) -> p n j", j=PACK),
+                w4_raw[:, :, lo:hi].rearrange("p j n -> p n j"), 1.0, 0.0, ALU.mult, ALU.add)
+            nc.vector.quantize_mx(out=w4_w[:, lo:hi].bitcast(FP8X4), scales=w4_sc[:, lo:hi],
+                                  in_=w4_bf[:, lo * PACK : hi * PACK])
+
+        out_v = out.rearrange("(g e p) m -> g p e m", e=2, p=P)
+        for half in range(2):
+            lo, hi = half * HALF, (half + 1) * HALF
+            for t in range(2, PACK):
+                nc.scalar.activation(edges23[:, t - 2, lo:hi], h[t][:].indirect(p1[:, lo // 16 : hi // 16]), ACT.Exp,
+                                     bias=bias_col(t), scale=temp_c[:, t : t + 1])
+                nc.vector.scalar_tensor_tensor(larger[:, t, lo:hi], faces23[:, t - 2, lo:hi], lean_c[:, t : t + 1],
+                                               edges23[:, t - 2, lo:hi], ALU.add, ALU.max)
+            weigh(1, lo, hi)
+            nc.vector.quantize_mx(out=m_w[:, lo:hi].bitcast(FP8X4), scales=m_sc[:, lo:hi],
+                                  in_=m_bf[:, lo * PACK : hi * PACK])
+        for half in range(2):
+            lo, hi = half * HALF, (half + 1) * HALF
+            for g in range(N // (2 * P)):
+                z = psum.tile([P, 2, HALF], F32, name="z", tag="second")
+                y = psum.tile([P, 2, HALF], F32, name="y", tag="first")
+                for e in range(2):
+                    n_cols = rows(2 * g + e)
+                    nc.tensor.matmul_mx(z[:, e, :], lhsT=w5_w[:, n_cols].bitcast(FP4X4), lhsT_scale=w5_sc[:, n_cols],
+                                        rhs=m_w[:, lo:hi].bitcast(FP8X4), rhs_scale=m_sc[:, lo:hi],
+                                        start=True, stop=True)
+                for e in range(2):
+                    n_cols = rows(2 * g + e)
+                    nc.tensor.matmul_mx(y[:, e, :], lhsT=w4_w[:, n_cols].bitcast(FP8X4), lhsT_scale=w4_sc[:, n_cols],
+                                        rhs=m_w[:, lo:hi].bitcast(FP8X4), rhs_scale=m_sc[:, lo:hi],
+                                        start=True, stop=True)
+                square = sbuf([P, 2, HALF], F32, f"square{half}_{g}")
+                nc.scalar.activation(square[:], z[:], ACT.Square)
+                result = sbuf([P, 2, HALF], F32, f"result{half}_{g}")
+                nc.vector.tensor_tensor(result[:], y[:], square[:], ALU.subtract)
+                nc.sync.dma_start(out=out_v[g][:, :, lo:hi], in_=result[:])

@@ -32,7 +32,7 @@ def tile_list_sculpture_jury_scores_kernel(
     nc = tc.nc
     with ExitStack() as ctx:
         sb = ctx.enter_context(tc.tile_pool(name="sb", bufs=1))
-        psum = ctx.enter_context(tc.psum_pool(name="psum", bufs=4))
+        psum = ctx.enter_context(tc.psum_pool(name="psum", bufs=1))
 
         def sbuf(shape, dtype, name, tag=""):
             return sb.tile(shape, dtype, name=name, tag=tag or name, align_bytes=64)
@@ -40,13 +40,12 @@ def tile_list_sculpture_jury_scores_kernel(
         tab_sc = sbuf([P, T], U8, "tab_sc")
         w3_sc_raw = sbuf([P, H], U8, "w3_sc_raw")
         w2_sc_raw = sbuf([P, PASSES, H], U8, "w2_sc_raw")
-        v_sc1 = sbuf([P, S], U8, "v_sc1")
         w5_sc = sbuf([P, N], U8, "w5_sc")
-        nc.gpsimd.memset(tab_sc[:].bitcast(I32), 0)
-        nc.vector.memset(w3_sc_raw[:].bitcast(I32), 0)
+        nc.gpsimd.memset(tab_sc[:, : T // 2].bitcast(I32), 0)
+        nc.vector.memset(tab_sc[:, T // 2 :].bitcast(I32), 0)
+        nc.gpsimd.memset(w3_sc_raw[:].bitcast(I32), 0)
         nc.vector.memset(w2_sc_raw[:].bitcast(I32), 0)
-        nc.gpsimd.memset(v_sc1[:].bitcast(I32), 0)
-        nc.gpsimd.memset(w5_sc[:].bitcast(I32), 0)
+        nc.vector.memset(w5_sc[:].bitcast(I32), 0)
 
         tab_w = [sbuf([P, T], U32, f"tab_w{a}") for a in range(PASSES)]
         w3_raw = [sbuf([P, H], U32, f"w3_raw{a}") for a in range(PASSES)]
@@ -65,26 +64,29 @@ def tile_list_sculpture_jury_scores_kernel(
         def load_words(dst, src):
             nc.sync.dma_start(out=dst[:].bitcast(I32), in_=src.rearrange("p c i -> p (c i)").bitcast(I32))
 
-        load_words(tab_w[0], tab_words[0])
+        def load_w1(a):
+            nc.sync.dma_start(out=w1_raw[a][:],
+                              in_=w1[a * 512 : (a + 1) * 512, :].rearrange("(p j) c -> p j c", j=PACK))
+
         nc.sync.dma_start(idx[:], offs)
+        nc.sync.dma_start(p1[:], pos1)
+        nc.sync.dma_start(p2[:], pos2)
         for q in range(QUADS):
             nc.sync.dma_start(out=tab_sc[32 * q : 32 * q + 8, :].bitcast(I32),
                               in_=tab_scales[:, 4 * q : 4 * q + 4, :].bitcast(I32))
-        load_words(w3_raw[0], w3_words[0])
+        load_words(tab_w[0], tab_words[0])
         for q in range(QUADS):
             nc.sync.dma_start(out=w3_sc_raw[32 * q : 32 * q + 8, :].bitcast(I32),
                               in_=w3_scales[:, 4 * q : 4 * q + 4, :].bitcast(I32))
+        load_words(w3_raw[0], w3_words[0])
         load_words(tab_w[1], tab_words[1])
+        load_words(w3_raw[1], w3_words[1])
+        nc.sync.dma_start(out=w2_raw[:].bitcast(I32), in_=w2_words.rearrange("a p c -> p a c").bitcast(I32))
         for q in range(QUADS):
             nc.sync.dma_start(out=w2_sc_raw[32 * q : 32 * q + 4, :, :].bitcast(I32),
                               in_=w2_scales[:, 4 * q : 4 * q + 4, :].rearrange("a r c -> r a c").bitcast(I32))
-        nc.sync.dma_start(out=w2_raw[:].bitcast(I32), in_=w2_words.rearrange("a p c -> p a c").bitcast(I32))
-        load_words(w3_raw[1], w3_words[1])
-        for a in range(PASSES):
-            nc.sync.dma_start(out=w1_raw[a][:],
-                              in_=w1[a * 512 : (a + 1) * 512, :].rearrange("(p j) c -> p j c", j=PACK))
-        nc.sync.dma_start(p1[:], pos1)
-        nc.sync.dma_start(p2[:], pos2)
+        load_w1(0)
+        load_w1(1)
         for dst, src in ((temp_c, temp), (thr_c, thr), (lean_c, lean)):
             nc.sync.dma_start(out=dst[:], in_=src.rearrange("(p t) -> p t", t=PACK))
         nc.sync.dma_start(out=w4_raw[:], in_=w4.rearrange("(p j) n -> p j n", j=PACK))
@@ -113,23 +115,22 @@ def tile_list_sculpture_jury_scores_kernel(
         def natural(ap):
             return ap.rearrange("p (m t) -> p m t", t=PACK)
 
-        nc.vector.tensor_copy(v_sc[:, cols(0)], tab_sc[:].indirect(entries(0)))
-        nc.vector.tensor_copy(v_w[0][:, cols(0)], tab_w[0][:].indirect(entries(0)))
-        nc.vector.tensor_copy(v_sc[:, cols(1)], tab_sc[:].indirect(entries(1)))
-        nc.vector.tensor_copy(v_w[0][:, cols(1)], tab_w[0][:].indirect(entries(1)))
-        for half in range(2):
-            nc.vector.tensor_copy(v_w[1][:, cols(half)], tab_w[1][:].indirect(entries(half)))
+        nc.vector.tensor_copy(v_sc[:], tab_sc[:].indirect(idx[:]))
+        for a in range(PASSES):
+            for half in range(2):
+                nc.vector.tensor_copy(v_w[a][:, cols(half)], tab_w[a][:].indirect(entries(half)))
+        for a in range(PASSES):
+            nc.vector.tensor_copy(dealt(w2_sc[:, a, :]), natural(w2_sc_raw[:, a, :]))
         nc.scalar.copy(dealt(w3_w[0][:]), natural(w3_raw[0][:]))
         nc.gpsimd.tensor_copy(w3_sc[:].rearrange("p (t m) -> p t m", t=PACK),
                               w3_sc_raw[:].rearrange("p (m t) -> p t m", t=PACK))
-        for a in range(PASSES):
-            nc.gpsimd.tensor_copy(w2_sc[:, a, :].rearrange("p (t m) -> p t m", t=PACK),
-                                  w2_sc_raw[:, a, :].rearrange("p (m t) -> p t m", t=PACK))
+        nc.scalar.copy(dealt(w3_w[1][:]), natural(w3_raw[1][:]))
+        v_sc1 = sbuf([P, S], U8, "v_sc1", tag="w3_raw1")
+        nc.gpsimd.memset(v_sc1[:].bitcast(I32), 0)
         for q in range(QUADS):
             nc.scalar.dma_start(out=v_sc1[32 * q : 32 * q + 4, :].bitcast(I32),
                                 in_=v_sc[32 * q + 4 : 32 * q + 8, :].bitcast(I32))
         nc.scalar.copy(dealt(w2_w[:, 0, :]), natural(w2_raw[:, 0, :]))
-        nc.scalar.copy(dealt(w3_w[1][:]), natural(w3_raw[1][:]))
         nc.scalar.copy(dealt(w2_w[:, 1, :]), natural(w2_raw[:, 1, :]))
 
         w1_w = [sbuf([P, H], U32, f"w1_w{a}") for a in range(PASSES)]
@@ -145,21 +146,21 @@ def tile_list_sculpture_jury_scores_kernel(
         def rows(t):
             return slice(t * P, (t + 1) * P)
 
-        def pass_w3(acc, t, half, a, start):
+        def pass_w3(acc, t, half, a, start=False, stop=False):
             nc.tensor.matmul_mx(acc[:], lhsT=w3_w[a][:, rows(t)].bitcast(FP8X4), lhsT_scale=w3_sc[4 * a :, rows(t)],
                                 rhs=v_w[a][:, cols(half)].bitcast(FP8X4), rhs_scale=v_sc[4 * a :, cols(half)],
-                                start=start, stop=False)
+                                start=start, stop=stop)
 
-        def pass_w1(acc, t, half, a, stop):
+        def pass_w1(acc, t, half, a, start=False, stop=False):
             nc.tensor.matmul_mx(acc[:], lhsT=w1_w[a][:, rows(t)].bitcast(FP8X4), lhsT_scale=w1_sc[a][:, rows(t)],
                                 rhs=v_w[a][:, cols(half)].bitcast(FP8X4), rhs_scale=v_sc[4 * a :, cols(half)],
-                                start=False, stop=stop)
+                                start=start, stop=stop)
 
-        def pass_w2(acc, t, half, a, stop):
+        def pass_w2(acc, t, half, a, start=False, stop=False):
             plane = (v_sc, v_sc1)[a]
             nc.tensor.matmul_mx(acc[:], lhsT=w2_w[:, a, rows(t)].bitcast(FP4X4), lhsT_scale=w2_sc[:, a, rows(t)],
                                 rhs=v_w[a][:, cols(half)].bitcast(FP8X4), rhs_scale=plane[:, cols(half)],
-                                start=False, stop=stop)
+                                start=start, stop=stop)
 
         h = [sbuf([P, S], F32, f"h{t}") for t in range(PACK)]
         top = sbuf([P, PACK], F32, "top")
@@ -171,7 +172,10 @@ def tile_list_sculpture_jury_scores_kernel(
 
         def join(t, half, acc13, acc23):
             other = sbuf([P, BANK], F32, f"sum23_{t}_{half}")
-            nc.scalar.activation(other[:], acc23[:], ACT.Copy)
+            if t < 2:
+                nc.scalar.copy(other[:], acc23[:])
+            else:
+                nc.vector.tensor_copy(other[:], acc23[:])
             nc.vector.tensor_tensor(h[t][:, cols(half)], acc13[:], other[:], ALU.max)
 
         def row_max(t):
@@ -181,42 +185,38 @@ def tile_list_sculpture_jury_scores_kernel(
         acc13, acc23 = {}, {}
         for half in range(2):
             for t in range(2):
-                acc13[t, half] = psum.tile([P, BANK], F32, name="acc13", tag="first")
-                acc23[t, half] = psum.tile([P, BANK], F32, name="acc23", tag="second")
-                pass_w3(acc13[t, half], t, half, 0, True)
-                pass_w3(acc23[t, half], t, half, 0, True)
-        for half in range(2):
-            for t in range(2):
-                pass_w2(acc23[t, half], t, half, 0, False)
-        for half in range(2):
-            for t in range(2):
-                pass_w3(acc13[t, half], t, half, 1, False)
-                pass_w3(acc23[t, half], t, half, 1, False)
-        for t in range(2):
-            for half in range(2):
-                pass_w2(acc23[t, half], t, half, 1, True)
+                acc13[t, half] = psum.tile([P, BANK], F32, name="acc13", tag=f"bank{4 * t + 2 * half}")
+                acc23[t, half] = psum.tile([P, BANK], F32, name="acc23", tag=f"bank{4 * t + 2 * half + 1}")
+                pass_w3(acc13[t, half], t, half, 0, start=True)
+                pass_w3(acc23[t, half], t, half, 0, start=True)
         edges01 = sbuf([P, 2, M], F32, "edges01")
         for t in range(2):
             for half in range(2):
-                pass_w1(acc13[t, half], t, half, 0, False)
+                pass_w3(acc13[t, half], t, half, 1)
+                pass_w3(acc23[t, half], t, half, 1)
             for half in range(2):
-                pass_w1(acc13[t, half], t, half, 1, True)
+                pass_w2(acc23[t, half], t, half, 0)
+                pass_w2(acc23[t, half], t, half, 1, stop=True)
+            for half in range(2):
+                pass_w1(acc13[t, half], t, half, 0)
+            for half in range(2):
+                pass_w1(acc13[t, half], t, half, 1, stop=True)
                 join(t, half, acc13[t, half], acc23[t, half])
             row_max(t)
             nc.scalar.activation(edges01[:, t, :], h[t][:].indirect(p1[:]), ACT.Exp,
                                  bias=bias_col(t), scale=temp_c[:, t : t + 1])
         for t in range(2, PACK):
             for half in range(2):
-                b = psum.tile([P, BANK], F32, name="acc23", tag="second")
-                pass_w3(b, t, half, 0, True)
-                pass_w2(b, t, half, 0, False)
-                pass_w3(b, t, half, 1, False)
-                pass_w2(b, t, half, 1, True)
-                c = psum.tile([P, BANK], F32, name="acc13", tag="first")
-                pass_w3(c, t, half, 0, True)
-                pass_w3(c, t, half, 1, False)
-                pass_w1(c, t, half, 0, False)
-                pass_w1(c, t, half, 1, True)
+                b = psum.tile([P, BANK], F32, name="acc23", tag=f"bank{4 * (t - 2) + 2 * half}")
+                pass_w3(b, t, half, 0, start=True)
+                pass_w2(b, t, half, 0)
+                pass_w3(b, t, half, 1)
+                pass_w2(b, t, half, 1, stop=True)
+                c = psum.tile([P, BANK], F32, name="acc13", tag=f"bank{4 * (t - 2) + 2 * half + 1}")
+                pass_w1(c, t, half, 1, start=True)
+                pass_w1(c, t, half, 0)
+                pass_w3(c, t, half, 0)
+                pass_w3(c, t, half, 1, stop=True)
                 join(t, half, c, b)
             row_max(t)
 
@@ -231,20 +231,20 @@ def tile_list_sculpture_jury_scores_kernel(
         m_bf = sbuf([P, M * PACK], BF16, "m_bf")
         m_w = sbuf([P, M], U32, "m_w")
         m_sc = sbuf([P, M], U8, "m_sc")
-        larger = sbuf([P, PACK, M], F32, "larger")
 
-        def weigh(pair, lo, hi):
+        def weigh(pair, larger, lo, hi):
             dst = m_bf[:, lo * PACK : hi * PACK].rearrange("p (c i t) -> p c t i", i=4, t=PACK)
             nc.vector.tensor_tensor(
                 dst[:, :, 2 * pair : 2 * pair + 2, :],
-                larger[:, 2 * pair : 2 * pair + 2, lo:hi].rearrange("p t (c i) -> p c t i", i=4),
+                larger[:].rearrange("p t (c i) -> p c t i", i=4),
                 chair_sb[:, 2 * pair : 2 * pair + 2, lo:hi].rearrange("p t (c i) -> p c t i", i=4),
                 ALU.mult)
 
+        larger01 = sbuf([P, 2, M], F32, "larger01")
         for t in range(2):
-            nc.vector.scalar_tensor_tensor(larger[:, t, :], faces01[:, t, :], lean_c[:, t : t + 1], edges01[:, t, :],
+            nc.vector.scalar_tensor_tensor(larger01[:, t, :], faces01[:, t, :], lean_c[:, t : t + 1], edges01[:, t, :],
                                            ALU.add, ALU.max)
-        weigh(0, 0, M)
+        weigh(0, larger01, 0, M)
 
         w4_bf = sbuf([P, N * PACK], BF16, "w4_bf")
         w4_w = sbuf([P, N], U32, "w4_w")
@@ -260,19 +260,21 @@ def tile_list_sculpture_jury_scores_kernel(
         out_v = out.rearrange("(g e p) m -> g p e m", e=2, p=P)
         for half in range(2):
             lo, hi = half * HALF, (half + 1) * HALF
+            larger23 = sbuf([P, 2, HALF], F32, "larger23")
             for t in range(2, PACK):
                 nc.scalar.activation(edges23[:, t - 2, lo:hi], h[t][:].indirect(p1[:, lo // 16 : hi // 16]), ACT.Exp,
                                      bias=bias_col(t), scale=temp_c[:, t : t + 1])
-                nc.vector.scalar_tensor_tensor(larger[:, t, lo:hi], faces23[:, t - 2, lo:hi], lean_c[:, t : t + 1],
+                nc.vector.scalar_tensor_tensor(larger23[:, t - 2, :], faces23[:, t - 2, lo:hi], lean_c[:, t : t + 1],
                                                edges23[:, t - 2, lo:hi], ALU.add, ALU.max)
-            weigh(1, lo, hi)
+            weigh(1, larger23, lo, hi)
             nc.vector.quantize_mx(out=m_w[:, lo:hi].bitcast(FP8X4), scales=m_sc[:, lo:hi],
                                   in_=m_bf[:, lo * PACK : hi * PACK])
         for half in range(2):
             lo, hi = half * HALF, (half + 1) * HALF
             for g in range(N // (2 * P)):
-                z = psum.tile([P, 2, HALF], F32, name="z", tag="second")
-                y = psum.tile([P, 2, HALF], F32, name="y", tag="first")
+                step = half * (N // (2 * P)) + g
+                z = psum.tile([P, 2, HALF], F32, name="z", tag=f"bank{2 * step % 8}")
+                y = psum.tile([P, 2, HALF], F32, name="y", tag=f"bank{(2 * step + 1) % 8}")
                 for e in range(2):
                     n_cols = rows(2 * g + e)
                     nc.tensor.matmul_mx(z[:, e, :], lhsT=w5_w[:, n_cols].bitcast(FP4X4), lhsT_scale=w5_sc[:, n_cols],

@@ -23,6 +23,8 @@ PASSES = K // (P * PACK)
 BANK = 512
 QUADS = 4
 VECTOR_SHARE = 80
+W4_PIECE = 96
+LAST_STEP = 5
 
 
 def tile_list_sculpture_jury_scores_kernel(
@@ -40,26 +42,23 @@ def tile_list_sculpture_jury_scores_kernel(
         tab_sc = sbuf([P, T], U8, "tab_sc")
         w3_sc_raw = sbuf([P, H], U8, "w3_sc_raw")
         w2_sc_raw = sbuf([P, PASSES, H], U8, "w2_sc_raw")
-        w5_sc = sbuf([P, N], U8, "w5_sc")
         nc.gpsimd.memset(tab_sc[:, : T // 2].bitcast(I32), 0)
         nc.vector.memset(tab_sc[:, T // 2 :].bitcast(I32), 0)
         nc.gpsimd.memset(w3_sc_raw[:].bitcast(I32), 0)
         nc.vector.memset(w2_sc_raw[:].bitcast(I32), 0)
-        nc.vector.memset(w5_sc[:].bitcast(I32), 0)
+        v_sc1 = sbuf([P, S], U8, "v_sc1")
+        nc.gpsimd.memset(v_sc1[:].bitcast(I32), 0)
 
         tab_w = [sbuf([P, T], U32, f"tab_w{a}") for a in range(PASSES)]
         w3_raw = [sbuf([P, H], U32, f"w3_raw{a}") for a in range(PASSES)]
         w2_raw = sbuf([P, PASSES, H], U16, "w2_raw")
-        w1_raw = [sbuf([P, PACK, H], F32, f"w1_raw{a}") for a in range(PASSES)]
+        w1_raw = {0: sbuf([P, PACK, H], F32, "w1_raw0")}
         idx = sbuf([P, S // 16], U16, "idx")
         p1 = sbuf([P, M // 16], U16, "p1")
         p2 = sbuf([P, M // 16], U16, "p2")
         temp_c = sbuf([P, PACK], F32, "temp_c")
         thr_c = sbuf([P, PACK], F32, "thr_c", tag="thr_then_edges")
         lean_c = sbuf([P, PACK], F32, "lean_c")
-        chair_sb = sbuf([P, PACK, M], F32, "chair_sb")
-        w4_raw = sbuf([P, PACK, N], F32, "w4_raw")
-        w5_w = sbuf([P, N], U16, "w5_w")
 
         def load_words(dst, src):
             nc.sync.dma_start(out=dst[:].bitcast(I32), in_=src.rearrange("p c i -> p (c i)").bitcast(I32))
@@ -75,29 +74,26 @@ def tile_list_sculpture_jury_scores_kernel(
             nc.sync.dma_start(out=tab_sc[32 * q : 32 * q + 8, :].bitcast(I32),
                               in_=tab_scales[:, 4 * q : 4 * q + 4, :].bitcast(I32))
         load_words(tab_w[0], tab_words[0])
+        load_words(w3_raw[0], w3_words[0])
         for q in range(QUADS):
             nc.sync.dma_start(out=w3_sc_raw[32 * q : 32 * q + 8, :].bitcast(I32),
                               in_=w3_scales[:, 4 * q : 4 * q + 4, :].bitcast(I32))
-        load_words(w3_raw[0], w3_words[0])
-        load_words(tab_w[1], tab_words[1])
-        load_words(w3_raw[1], w3_words[1])
+        load_w1(0)
         nc.sync.dma_start(out=w2_raw[:].bitcast(I32), in_=w2_words.rearrange("a p c -> p a c").bitcast(I32))
         for q in range(QUADS):
             nc.sync.dma_start(out=w2_sc_raw[32 * q : 32 * q + 4, :, :].bitcast(I32),
                               in_=w2_scales[:, 4 * q : 4 * q + 4, :].rearrange("a r c -> r a c").bitcast(I32))
-        load_w1(0)
-        load_w1(1)
-        for dst, src in ((temp_c, temp), (thr_c, thr), (lean_c, lean)):
-            nc.sync.dma_start(out=dst[:], in_=src.rearrange("(p t) -> p t", t=PACK))
-        nc.sync.dma_start(out=w4_raw[:], in_=w4.rearrange("(p j) n -> p j n", j=PACK))
-        nc.sync.dma_start(out=chair_sb[:], in_=chair.rearrange("(p t) m -> p t m", t=PACK))
-        nc.sync.dma_start(out=w5_w[:].bitcast(I32), in_=w5_words[0].bitcast(I32))
+        load_words(tab_w[1], tab_words[1])
+        load_words(w3_raw[1], w3_words[1])
+        v_sc = sbuf([P, S], U8, "v_sc")
+        nc.vector.tensor_copy(v_sc[:], tab_sc[:].indirect(idx[:]))
         for q in range(QUADS):
-            nc.sync.dma_start(out=w5_sc[32 * q : 32 * q + 4, :].bitcast(I32),
-                              in_=w5_scales[0, 4 * q : 4 * q + 4, :].bitcast(I32))
+            nc.sync.dma_start(out=v_sc1[32 * q : 32 * q + 4, :].bitcast(I32),
+                              in_=v_sc[32 * q + 4 : 32 * q + 8, :].bitcast(I32))
+        for dst, src in ((temp_c, temp), (thr_c, thr), (lean_c, lean)):
+            nc.gpsimd.dma_start(out=dst[:], in_=src.rearrange("(p t) -> p t", t=PACK))
 
         v_w = [sbuf([P, S], U32, f"v_w{a}") for a in range(PASSES)]
-        v_sc = sbuf([P, S], U8, "v_sc")
         w3_w = [sbuf([P, H], U32, f"w3_w{a}") for a in range(PASSES)]
         w2_w = sbuf([P, PASSES, H], U16, "w2_w")
         w3_sc = sbuf([P, H], U8, "w3_sc")
@@ -115,33 +111,52 @@ def tile_list_sculpture_jury_scores_kernel(
         def natural(ap):
             return ap.rearrange("p (m t) -> p m t", t=PACK)
 
-        nc.vector.tensor_copy(v_sc[:], tab_sc[:].indirect(idx[:]))
-        for a in range(PASSES):
-            for half in range(2):
-                nc.vector.tensor_copy(v_w[a][:, cols(half)], tab_w[a][:].indirect(entries(half)))
-        for a in range(PASSES):
-            nc.vector.tensor_copy(dealt(w2_sc[:, a, :]), natural(w2_sc_raw[:, a, :]))
-        nc.scalar.copy(dealt(w3_w[0][:]), natural(w3_raw[0][:]))
-        nc.gpsimd.tensor_copy(w3_sc[:].rearrange("p (t m) -> p t m", t=PACK),
-                              w3_sc_raw[:].rearrange("p (m t) -> p t m", t=PACK))
-        nc.scalar.copy(dealt(w3_w[1][:]), natural(w3_raw[1][:]))
-        v_sc1 = sbuf([P, S], U8, "v_sc1", tag="w3_raw1")
-        nc.gpsimd.memset(v_sc1[:].bitcast(I32), 0)
-        for q in range(QUADS):
-            nc.scalar.dma_start(out=v_sc1[32 * q : 32 * q + 4, :].bitcast(I32),
-                                in_=v_sc[32 * q + 4 : 32 * q + 8, :].bitcast(I32))
-        nc.scalar.copy(dealt(w2_w[:, 0, :]), natural(w2_raw[:, 0, :]))
-        nc.scalar.copy(dealt(w2_w[:, 1, :]), natural(w2_raw[:, 1, :]))
-
         w1_w = [sbuf([P, H], U32, f"w1_w{a}") for a in range(PASSES)]
         w1_sc = [sbuf([P, H], U8, f"w1_sc{a}") for a in range(PASSES)]
-        for a in range(PASSES):
+
+        def gather_words(a):
+            for half in range(2):
+                nc.vector.tensor_copy(v_w[a][:, cols(half)], tab_w[a][:].indirect(entries(half)))
+
+        def quantise_w1(a):
             w1_bf = sbuf([P, H * PACK], BF16, f"w1_bf{a}")
             dst = w1_bf[:].rearrange("p (t m j) -> p m j t", t=PACK, j=PACK)
             src = w1_raw[a][:].rearrange("p j (m t) -> p m j t", t=PACK)
-            nc.vector.tensor_copy(dst[:, :VECTOR_SHARE], src[:, :VECTOR_SHARE])
-            nc.scalar.activation(dst[:, VECTOR_SHARE:], src[:, VECTOR_SHARE:], ACT.Copy)
-            nc.vector.quantize_mx(out=w1_w[a][:].bitcast(FP8X4), scales=w1_sc[a][:], in_=w1_bf[:])
+            share = (VECTOR_SHARE, P)[a]
+            nc.vector.tensor_copy(dst[:, :share], src[:, :share])
+            if share < P:
+                nc.scalar.activation(dst[:, share:], src[:, share:], ACT.Copy)
+            for lo in (0, H // 2):
+                hi = lo + H // 2
+                nc.vector.quantize_mx(out=w1_w[a][:, lo:hi].bitcast(FP8X4), scales=w1_sc[a][:, lo:hi],
+                                      in_=w1_bf[:, lo * PACK : hi * PACK])
+
+        gather_words(0)
+        nc.scalar.copy(dealt(w3_w[0][:]), natural(w3_raw[0][:]))
+        w1_raw[1] = sbuf([P, PACK, H], F32, "w1_raw1", tag="w3_raw0")
+        load_w1(1)
+        for t in (0, 2):
+            nc.gpsimd.tensor_copy(w3_sc[:].rearrange("p (t m) -> p t m", t=PACK)[:, t : t + 2],
+                                  w3_sc_raw[:].rearrange("p (m t) -> p t m", t=PACK)[:, t : t + 2])
+        quantise_w1(0)
+        w4_raw = sbuf([P, PACK, N], F32, "w4_raw", tag="w1_raw0")
+        nc.sync.dma_start(out=w4_raw[:], in_=w4.rearrange("(p j) n -> p j n", j=PACK))
+        nc.scalar.copy(dealt(w2_w[:, 0, :]), natural(w2_raw[:, 0, :]))
+        nc.vector.tensor_copy(dealt(w2_sc[:, 0, :]), natural(w2_sc_raw[:, 0, :]))
+        nc.scalar.copy(dealt(w2_w[:, 1, :]), natural(w2_raw[:, 1, :]))
+        nc.vector.tensor_copy(dealt(w2_sc[:, 1, :]), natural(w2_sc_raw[:, 1, :]))
+        chair_sb = sbuf([P, PACK, M], F32, "chair_sb", tag="w2_raw")
+        nc.sync.dma_start(out=chair_sb[:], in_=chair.rearrange("(p t) m -> p t m", t=PACK))
+        w5_sc = sbuf([P, N], U8, "w5_sc", tag="w2_sc_raw")
+        nc.vector.memset(w5_sc[:].bitcast(I32), 0)
+        for q in range(QUADS):
+            nc.sync.dma_start(out=w5_sc[32 * q : 32 * q + 4, :].bitcast(I32),
+                              in_=w5_scales[0, 4 * q : 4 * q + 4, :].bitcast(I32))
+        gather_words(1)
+        nc.scalar.copy(dealt(w3_w[1][:]), natural(w3_raw[1][:]))
+        w5_w = sbuf([P, N], U16, "w5_w", tag="w3_raw1")
+        nc.sync.dma_start(out=w5_w[:].bitcast(I32), in_=w5_words[0].bitcast(I32))
+        quantise_w1(1)
 
         def rows(t):
             return slice(t * P, (t + 1) * P)
@@ -172,7 +187,7 @@ def tile_list_sculpture_jury_scores_kernel(
 
         def join(t, half, acc13, acc23):
             other = sbuf([P, BANK], F32, f"sum23_{t}_{half}")
-            if t < 2:
+            if t < 3:
                 nc.scalar.copy(other[:], acc23[:])
             else:
                 nc.vector.tensor_copy(other[:], acc23[:])
@@ -192,13 +207,20 @@ def tile_list_sculpture_jury_scores_kernel(
         edges01 = sbuf([P, 2, M], F32, "edges01")
         for t in range(2):
             for half in range(2):
-                pass_w3(acc13[t, half], t, half, 1)
-                pass_w3(acc23[t, half], t, half, 1)
+                pass_w1(acc13[t, half], t, half, 0)
+        for t in range(2):
             for half in range(2):
                 pass_w2(acc23[t, half], t, half, 0)
-                pass_w2(acc23[t, half], t, half, 1, stop=True)
-            for half in range(2):
-                pass_w1(acc13[t, half], t, half, 0)
+
+        def second_passes(t, half):
+            pass_w3(acc23[t, half], t, half, 1)
+            pass_w2(acc23[t, half], t, half, 1, stop=True)
+            pass_w3(acc13[t, half], t, half, 1)
+
+        for t in range(2):
+            second_passes(t, 0)
+        for t in range(2):
+            second_passes(t, 1)
             for half in range(2):
                 pass_w1(acc13[t, half], t, half, 1, stop=True)
                 join(t, half, acc13[t, half], acc23[t, half])
@@ -240,7 +262,7 @@ def tile_list_sculpture_jury_scores_kernel(
                 chair_sb[:, 2 * pair : 2 * pair + 2, lo:hi].rearrange("p t (c i) -> p c t i", i=4),
                 ALU.mult)
 
-        larger01 = sbuf([P, 2, M], F32, "larger01")
+        larger01 = sbuf([P, 2, M], F32, "larger01", tag="sum23_3_1")
         for t in range(2):
             nc.vector.scalar_tensor_tensor(larger01[:, t, :], faces01[:, t, :], lean_c[:, t : t + 1], edges01[:, t, :],
                                            ALU.add, ALU.max)
@@ -251,9 +273,11 @@ def tile_list_sculpture_jury_scores_kernel(
         w4_sc = sbuf([P, N], U8, "w4_sc")
         for g in range(2):
             lo, hi = g * N // 2, (g + 1) * N // 2
-            nc.gpsimd.tensor_scalar(
-                w4_bf[:, lo * PACK : hi * PACK].rearrange("p (n j) -> p n j", j=PACK),
-                w4_raw[:, :, lo:hi].rearrange("p j n -> p n j"), 1.0, 0.0, ALU.mult, ALU.add)
+            for c0 in range(lo, hi, W4_PIECE):
+                c1 = c0 + W4_PIECE
+                nc.gpsimd.tensor_scalar(
+                    w4_bf[:, c0 * PACK : c1 * PACK].rearrange("p (n j) -> p n j", j=PACK),
+                    w4_raw[:, :, c0:c1].rearrange("p j n -> p n j"), 1.0, 0.0, ALU.mult, ALU.add)
             nc.vector.quantize_mx(out=w4_w[:, lo:hi].bitcast(FP8X4), scales=w4_sc[:, lo:hi],
                                   in_=w4_bf[:, lo * PACK : hi * PACK])
 
@@ -286,7 +310,9 @@ def tile_list_sculpture_jury_scores_kernel(
                                         rhs=m_w[:, lo:hi].bitcast(FP8X4), rhs_scale=m_sc[:, lo:hi],
                                         start=True, stop=True)
                 square = sbuf([P, 2, HALF], F32, f"square{half}_{g}")
-                nc.scalar.activation(square[:], z[:], ACT.Square)
                 result = sbuf([P, 2, HALF], F32, f"result{half}_{g}")
-                nc.vector.tensor_tensor(result[:], y[:], square[:], ALU.subtract)
-                nc.sync.dma_start(out=out_v[g][:, :, lo:hi], in_=result[:])
+                nc.scalar.activation(square[:], z[:], ACT.Square)
+                pieces = (slice(0, 1), slice(1, 2)) if step == LAST_STEP else (slice(0, 2),)
+                for piece in pieces:
+                    nc.vector.tensor_tensor(result[:, piece], y[:, piece], square[:, piece], ALU.subtract)
+                    nc.sync.dma_start(out=out_v[g][:, piece, lo:hi], in_=result[:, piece])

@@ -15,15 +15,14 @@ FP8X4 = mybir.dt.float8_e4m3fn_x4
 FP4X4 = mybir.dt.float4_e2m1fn_x4
 ACT = mybir.ActivationFunctionType
 ALU = mybir.AluOpType
-AX = mybir.AxisListType
 
 P = 128
 PACK = 4
 PASSES = K // (P * PACK)
 BANK = 512
 QUADS = 4
-VECTOR_SHARE = 80
-W4_PIECE = 96
+VECTOR_SHARES = (80, 64)
+W4_BLOCKS = (3, 2, 1)
 LAST_STEP = 5
 
 
@@ -122,10 +121,9 @@ def tile_list_sculpture_jury_scores_kernel(
             w1_bf = sbuf([P, H * PACK], BF16, f"w1_bf{a}")
             dst = w1_bf[:].rearrange("p (t m j) -> p m j t", t=PACK, j=PACK)
             src = w1_raw[a][:].rearrange("p j (m t) -> p m j t", t=PACK)
-            share = (VECTOR_SHARE, P)[a]
+            share = VECTOR_SHARES[a]
             nc.vector.tensor_copy(dst[:, :share], src[:, :share])
-            if share < P:
-                nc.scalar.activation(dst[:, share:], src[:, share:], ACT.Copy)
+            nc.scalar.activation(dst[:, share:], src[:, share:], ACT.Copy)
             for lo in (0, H // 2):
                 hi = lo + H // 2
                 nc.vector.quantize_mx(out=w1_w[a][:, lo:hi].bitcast(FP8X4), scales=w1_sc[a][:, lo:hi],
@@ -178,7 +176,10 @@ def tile_list_sculpture_jury_scores_kernel(
                                 start=start, stop=stop)
 
         h = [sbuf([P, S], F32, f"h{t}") for t in range(PACK)]
-        top = sbuf([P, PACK], F32, "top")
+        first_sums = sbuf([P, 4, BANK], F32, "first_sums", tag="w3_raw0")
+        neg_temp = sbuf([P, PACK], F32, "neg_temp")
+        nc.gpsimd.tensor_scalar(neg_temp[:], temp_c[:], -1.0, 0.0, ALU.mult, ALU.add)
+        scaled = sbuf([P, S], F32, "scaled")
         bias01 = sbuf([P, 2], F32, "bias01", tag="bias_then_faces")
         bias23 = sbuf([P, 2], F32, "bias23")
 
@@ -186,16 +187,19 @@ def tile_list_sculpture_jury_scores_kernel(
             return (bias01, bias23)[t // 2][:, t % 2 : t % 2 + 1]
 
         def join(t, half, acc13, acc23):
-            other = sbuf([P, BANK], F32, f"sum23_{t}_{half}")
-            if t < 3:
-                nc.scalar.copy(other[:], acc23[:])
+            if t < 2:
+                other = first_sums[:, 2 * t + half, :]
             else:
-                nc.vector.tensor_copy(other[:], acc23[:])
-            nc.vector.tensor_tensor(h[t][:, cols(half)], acc13[:], other[:], ALU.max)
+                other = sbuf([P, BANK], F32, f"sum23_{t}_{half}")[:]
+            if t < 3:
+                nc.scalar.copy(other, acc23[:])
+            else:
+                nc.vector.tensor_copy(other, acc23[:])
+            nc.vector.tensor_tensor(h[t][:, cols(half)], acc13[:], other, ALU.max)
 
         def row_max(t):
-            nc.vector.reduce_max(top[:, t : t + 1], h[t][:], AX.X)
-            nc.vector.tensor_scalar(bias_col(t), top[:, t : t + 1], temp_c[:, t : t + 1], -1.0, ALU.mult, ALU.mult)
+            nc.vector.tensor_scalar(scaled[:], h[t][:], neg_temp[:, t : t + 1], None, ALU.mult, ALU.min,
+                                    accum_out=bias_col(t))
 
         acc13, acc23 = {}, {}
         for half in range(2):
@@ -234,12 +238,14 @@ def tile_list_sculpture_jury_scores_kernel(
                 pass_w2(b, t, half, 0)
                 pass_w3(b, t, half, 1)
                 pass_w2(b, t, half, 1, stop=True)
+                acc23[t, half] = b
+            for half in range(2):
                 c = psum.tile([P, BANK], F32, name="acc13", tag=f"bank{4 * (t - 2) + 2 * half + 1}")
                 pass_w1(c, t, half, 1, start=True)
                 pass_w1(c, t, half, 0)
                 pass_w3(c, t, half, 0)
                 pass_w3(c, t, half, 1, stop=True)
-                join(t, half, c, b)
+                join(t, half, c, acc23[t, half])
             row_max(t)
 
         HALF = M // 2
@@ -269,17 +275,20 @@ def tile_list_sculpture_jury_scores_kernel(
         weigh(0, larger01, 0, M)
 
         w4_bf = sbuf([P, N * PACK], BF16, "w4_bf")
-        w4_w = sbuf([P, N], U32, "w4_w")
         w4_sc = sbuf([P, N], U8, "w4_sc")
-        for g in range(2):
-            lo, hi = g * N // 2, (g + 1) * N // 2
-            for c0 in range(lo, hi, W4_PIECE):
-                c1 = c0 + W4_PIECE
+        w4_blocks = []
+        lo = 0
+        for g, blocks in enumerate(W4_BLOCKS):
+            hi = lo + blocks * P
+            w4_w = sbuf([P, hi - lo], U32, f"w4_w{g}", tag="sum23_3_1" if hi == N else "")
+            for c0 in range(lo, hi, P):
                 nc.gpsimd.tensor_scalar(
-                    w4_bf[:, c0 * PACK : c1 * PACK].rearrange("p (n j) -> p n j", j=PACK),
-                    w4_raw[:, :, c0:c1].rearrange("p j n -> p n j"), 1.0, 0.0, ALU.mult, ALU.add)
-            nc.vector.quantize_mx(out=w4_w[:, lo:hi].bitcast(FP8X4), scales=w4_sc[:, lo:hi],
+                    w4_bf[:, c0 * PACK : (c0 + P) * PACK].rearrange("p (n j) -> p n j", j=PACK),
+                    w4_raw[:, :, c0 : c0 + P].rearrange("p j n -> p n j"), 1.0, 0.0, ALU.mult, ALU.add)
+                w4_blocks.append(w4_w[:, c0 - lo : c0 - lo + P])
+            nc.vector.quantize_mx(out=w4_w[:].bitcast(FP8X4), scales=w4_sc[:, lo:hi],
                                   in_=w4_bf[:, lo * PACK : hi * PACK])
+            lo = hi
 
         out_v = out.rearrange("(g e p) m -> g p e m", e=2, p=P)
         for half in range(2):
@@ -306,7 +315,7 @@ def tile_list_sculpture_jury_scores_kernel(
                                         start=True, stop=True)
                 for e in range(2):
                     n_cols = rows(2 * g + e)
-                    nc.tensor.matmul_mx(y[:, e, :], lhsT=w4_w[:, n_cols].bitcast(FP8X4), lhsT_scale=w4_sc[:, n_cols],
+                    nc.tensor.matmul_mx(y[:, e, :], lhsT=w4_blocks[2 * g + e].bitcast(FP8X4), lhsT_scale=w4_sc[:, n_cols],
                                         rhs=m_w[:, lo:hi].bitcast(FP8X4), rhs_scale=m_sc[:, lo:hi],
                                         start=True, stop=True)
                 square = sbuf([P, 2, HALF], F32, f"square{half}_{g}")

from contextlib import ExitStack

import concourse.mybir as mybir

K, T, S, M, H, N = 1024, 2048, 1024, 512, 512, 768
FLOPS = 2 * (4 * K * H * S + 2 * H * N * M)

F32 = mybir.dt.float32
BF16 = mybir.dt.bfloat16
I32 = mybir.dt.int32
U32 = mybir.dt.uint32
U16 = mybir.dt.uint16
U8 = mybir.dt.uint8
FP8X4 = mybir.dt.float8_e4m3fn_x4
FP4X4 = mybir.dt.float4_e2m1fn_x4
ACT = mybir.ActivationFunctionType
ALU = mybir.AluOpType

P = 128
PACK = 4
PASSES = K // (P * PACK)
BANK = 512
QUADS = 4
VECTOR_SHARES = (80, 64)
W4_BLOCKS = (3, 2, 1)
LAST_STEP = 5


def tile_list_sculpture_jury_scores_kernel(
    tc, tab_words, tab_scales, offs, pos1, pos2, w1, w2_words, w2_scales, w3_words, w3_scales,
    temp, thr, lean, chair, w4, w5_words, w5_scales, out,
):
    nc = tc.nc
    with ExitStack() as ctx:
        sb = ctx.enter_context(tc.tile_pool(name="sb", bufs=1))
        psum = ctx.enter_context(tc.psum_pool(name="psum", bufs=1))

        def sbuf(shape, dtype, name, tag=""):
            return sb.tile(shape, dtype, name=name, tag=tag or name, align_bytes=64)

        tab_sc = sbuf([P, T], U8, "tab_sc")
        w3_sc_raw = sbuf([P, H], U8, "w3_sc_raw")
        w2_sc_raw = sbuf([P, PASSES, H], U8, "w2_sc_raw")
        nc.gpsimd.memset(tab_sc[:, : T // 2].bitcast(I32), 0)
        nc.vector.memset(tab_sc[:, T // 2 :].bitcast(I32), 0)
        nc.gpsimd.memset(w3_sc_raw[:].bitcast(I32), 0)
        nc.vector.memset(w2_sc_raw[:].bitcast(I32), 0)
        v_sc1 = sbuf([P, S], U8, "v_sc1")
        nc.gpsimd.memset(v_sc1[:].bitcast(I32), 0)

        tab_w = [sbuf([P, T], U32, f"tab_w{a}") for a in range(PASSES)]
        w3_raw = [sbuf([P, H], U32, f"w3_raw{a}") for a in range(PASSES)]
        w2_raw = sbuf([P, PASSES, H], U16, "w2_raw")
        w1_raw = {0: sbuf([P, PACK, H], F32, "w1_raw0")}
        idx = sbuf([P, S // 16], U16, "idx")
        p1 = sbuf([P, M // 16], U16, "p1")
        p2 = sbuf([P, M // 16], U16, "p2")
        temp_c = sbuf([P, PACK], F32, "temp_c")
        thr_c = sbuf([P, PACK], F32, "thr_c", tag="thr_then_edges")
        lean_c = sbuf([P, PACK], F32, "lean_c")

        def load_words(dst, src):
            nc.sync.dma_start(out=dst[:].bitcast(I32), in_=src.rearrange("p c i -> p (c i)").bitcast(I32))

        def load_w1(a):
            nc.sync.dma_start(out=w1_raw[a][:],
                              in_=w1[a * 512 : (a + 1) * 512, :].rearrange("(p j) c -> p j c", j=PACK))

        nc.sync.dma_start(idx[:], offs)
        nc.sync.dma_start(p1[:], pos1)
        nc.sync.dma_start(p2[:], pos2)
        for q in range(QUADS):
            nc.sync.dma_start(out=tab_sc[32 * q : 32 * q + 8, :].bitcast(I32),
                              in_=tab_scales[:, 4 * q : 4 * q + 4, :].bitcast(I32))
        load_words(tab_w[0], tab_words[0])
        load_words(w3_raw[0], w3_words[0])
        for q in range(QUADS):
            nc.sync.dma_start(out=w3_sc_raw[32 * q : 32 * q + 8, :].bitcast(I32),
                              in_=w3_scales[:, 4 * q : 4 * q + 4, :].bitcast(I32))
        load_w1(0)
        nc.sync.dma_start(out=w2_raw[:].bitcast(I32), in_=w2_words.rearrange("a p c -> p a c").bitcast(I32))
        for q in range(QUADS):
            nc.sync.dma_start(out=w2_sc_raw[32 * q : 32 * q + 4, :, :].bitcast(I32),
                              in_=w2_scales[:, 4 * q : 4 * q + 4, :].rearrange("a r c -> r a c").bitcast(I32))
        load_words(tab_w[1], tab_words[1])
        load_words(w3_raw[1], w3_words[1])
        v_sc = sbuf([P, S], U8, "v_sc")
        nc.vector.tensor_copy(v_sc[:], tab_sc[:].indirect(idx[:]))
        for q in range(QUADS):
            nc.sync.dma_start(out=v_sc1[32 * q : 32 * q + 4, :].bitcast(I32),
                              in_=v_sc[32 * q + 4 : 32 * q + 8, :].bitcast(I32))
        for dst, src in ((temp_c, temp), (thr_c, thr), (lean_c, lean)):
            nc.gpsimd.dma_start(out=dst[:], in_=src.rearrange("(p t) -> p t", t=PACK))

        v_w = [sbuf([P, S], U32, f"v_w{a}") for a in range(PASSES)]
        w3_w = [sbuf([P, H], U32, f"w3_w{a}") for a in range(PASSES)]
        w2_w = sbuf([P, PASSES, H], U16, "w2_w")
        w3_sc = sbuf([P, H], U8, "w3_sc")
        w2_sc = sbuf([P, PASSES, H], U8, "w2_sc")

        def cols(half):
            return slice(half * BANK, (half + 1) * BANK)

        def entries(half):
            return idx[:, half * (BANK // 16) : (half + 1) * (BANK // 16)]

        def dealt(ap):
            return ap.rearrange("p (t m) -> p m t", t=PACK)

        def natural(ap):
            return ap.rearrange("p (m t) -> p m t", t=PACK)

        w1_w = [sbuf([P, H], U32, f"w1_w{a}") for a in range(PASSES)]
        w1_sc = [sbuf([P, H], U8, f"w1_sc{a}") for a in range(PASSES)]

        def gather_words(a):
            for half in range(2):
                nc.vector.tensor_copy(v_w[a][:, cols(half)], tab_w[a][:].indirect(entries(half)))

        def quantise_w1(a):
            w1_bf = sbuf([P, H * PACK], BF16, f"w1_bf{a}")
            dst = w1_bf[:].rearrange("p (t m j) -> p m j t", t=PACK, j=PACK)
            src = w1_raw[a][:].rearrange("p j (m t) -> p m j t", t=PACK)
            share = VECTOR_SHARES[a]
            nc.vector.tensor_copy(dst[:, :share], src[:, :share])
            nc.scalar.activation(dst[:, share:], src[:, share:], ACT.Copy)
            for lo in (0, H // 2):
                hi = lo + H // 2
                nc.vector.quantize_mx(out=w1_w[a][:, lo:hi].bitcast(FP8X4), scales=w1_sc[a][:, lo:hi],
                                      in_=w1_bf[:, lo * PACK : hi * PACK])

        gather_words(0)
        nc.scalar.copy(dealt(w3_w[0][:]), natural(w3_raw[0][:]))
        w1_raw[1] = sbuf([P, PACK, H], F32, "w1_raw1", tag="w3_raw0")
        load_w1(1)
        for t in (0, 2):
            nc.gpsimd.tensor_copy(w3_sc[:].rearrange("p (t m) -> p t m", t=PACK)[:, t : t + 2],
                                  w3_sc_raw[:].rearrange("p (m t) -> p t m", t=PACK)[:, t : t + 2])
        quantise_w1(0)
        w4_raw = sbuf([P, PACK, N], F32, "w4_raw", tag="w1_raw0")
        nc.sync.dma_start(out=w4_raw[:], in_=w4.rearrange("(p j) n -> p j n", j=PACK))
        nc.scalar.copy(dealt(w2_w[:, 0, :]), natural(w2_raw[:, 0, :]))
        nc.vector.tensor_copy(dealt(w2_sc[:, 0, :]), natural(w2_sc_raw[:, 0, :]))
        nc.scalar.copy(dealt(w2_w[:, 1, :]), natural(w2_raw[:, 1, :]))
        nc.vector.tensor_copy(dealt(w2_sc[:, 1, :]), natural(w2_sc_raw[:, 1, :]))
        chair_sb = sbuf([P, PACK, M], F32, "chair_sb", tag="w2_raw")
        nc.sync.dma_start(out=chair_sb[:], in_=chair.rearrange("(p t) m -> p t m", t=PACK))
        w5_sc = sbuf([P, N], U8, "w5_sc", tag="w2_sc_raw")
        nc.vector.memset(w5_sc[:].bitcast(I32), 0)
        for q in range(QUADS):
            nc.sync.dma_start(out=w5_sc[32 * q : 32 * q + 4, :].bitcast(I32),
                              in_=w5_scales[0, 4 * q : 4 * q + 4, :].bitcast(I32))
        gather_words(1)
        nc.scalar.copy(dealt(w3_w[1][:]), natural(w3_raw[1][:]))
        w5_w = sbuf([P, N], U16, "w5_w", tag="w3_raw1")
        nc.sync.dma_start(out=w5_w[:].bitcast(I32), in_=w5_words[0].bitcast(I32))
        quantise_w1(1)

        def rows(t):
            return slice(t * P, (t + 1) * P)

        def pass_w3(acc, t, half, a, start=False, stop=False):
            nc.tensor.matmul_mx(acc[:], lhsT=w3_w[a][:, rows(t)].bitcast(FP8X4), lhsT_scale=w3_sc[4 * a :, rows(t)],
                                rhs=v_w[a][:, cols(half)].bitcast(FP8X4), rhs_scale=v_sc[4 * a :, cols(half)],
                                start=start, stop=stop)

        def pass_w1(acc, t, half, a, start=False, stop=False):
            nc.tensor.matmul_mx(acc[:], lhsT=w1_w[a][:, rows(t)].bitcast(FP8X4), lhsT_scale=w1_sc[a][:, rows(t)],
                                rhs=v_w[a][:, cols(half)].bitcast(FP8X4), rhs_scale=v_sc[4 * a :, cols(half)],
                                start=start, stop=stop)

        def pass_w2(acc, t, half, a, start=False, stop=False):
            plane = (v_sc, v_sc1)[a]
            nc.tensor.matmul_mx(acc[:], lhsT=w2_w[:, a, rows(t)].bitcast(FP4X4), lhsT_scale=w2_sc[:, a, rows(t)],
                                rhs=v_w[a][:, cols(half)].bitcast(FP8X4), rhs_scale=plane[:, cols(half)],
                                start=start, stop=stop)

        h = [sbuf([P, S], F32, f"h{t}") for t in range(PACK)]
        first_sums = sbuf([P, 4, BANK], F32, "first_sums", tag="w3_raw0")
        neg_temp = sbuf([P, PACK], F32, "neg_temp")
        nc.gpsimd.tensor_scalar(neg_temp[:], temp_c[:], -1.0, 0.0, ALU.mult, ALU.add)
        scaled = sbuf([P, S], F32, "scaled")
        bias01 = sbuf([P, 2], F32, "bias01", tag="bias_then_faces")
        bias23 = sbuf([P, 2], F32, "bias23")

        def bias_col(t):
            return (bias01, bias23)[t // 2][:, t % 2 : t % 2 + 1]

        def join(t, half, acc13, acc23):
            if t < 2:
                other = first_sums[:, 2 * t + half, :]
            else:
                other = sbuf([P, BANK], F32, f"sum23_{t}_{half}")[:]
            if t < 3:
                nc.scalar.copy(other, acc23[:])
            else:
                nc.vector.tensor_copy(other, acc23[:])
            nc.vector.tensor_tensor(h[t][:, cols(half)], acc13[:], other, ALU.max)

        def row_max(t):
            nc.vector.tensor_scalar(scaled[:], h[t][:], neg_temp[:, t : t + 1], None, ALU.mult, ALU.min,
                                    accum_out=bias_col(t))

        acc13, acc23 = {}, {}
        for half in range(2):
            for t in range(2):
                acc13[t, half] = psum.tile([P, BANK], F32, name="acc13", tag=f"bank{4 * t + 2 * half}")
                acc23[t, half] = psum.tile([P, BANK], F32, name="acc23", tag=f"bank{4 * t + 2 * half + 1}")
                pass_w3(acc13[t, half], t, half, 0, start=True)
                pass_w3(acc23[t, half], t, half, 0, start=True)
        edges01 = sbuf([P, 2, M], F32, "edges01")
        for t in range(2):
            for half in range(2):
                pass_w1(acc13[t, half], t, half, 0)
        for t in range(2):
            for half in range(2):
                pass_w2(acc23[t, half], t, half, 0)

        def second_passes(t, half):
            pass_w3(acc23[t, half], t, half, 1)
            pass_w2(acc23[t, half], t, half, 1, stop=True)
            pass_w3(acc13[t, half], t, half, 1)

        for t in range(2):
            second_passes(t, 0)
        for t in range(2):
            second_passes(t, 1)
            for half in range(2):
                pass_w1(acc13[t, half], t, half, 1, stop=True)
                join(t, half, acc13[t, half], acc23[t, half])
            row_max(t)
            nc.scalar.activation(edges01[:, t, :], h[t][:].indirect(p1[:]), ACT.Exp,
                                 bias=bias_col(t), scale=temp_c[:, t : t + 1])
        for t in range(2, PACK):
            for half in range(2):
                b = psum.tile([P, BANK], F32, name="acc23", tag=f"bank{4 * (t - 2) + 2 * half}")
                pass_w3(b, t, half, 0, start=True)
                pass_w2(b, t, half, 0)
                pass_w3(b, t, half, 1)
                pass_w2(b, t, half, 1, stop=True)
                acc23[t, half] = b
            for half in range(2):
                c = psum.tile([P, BANK], F32, name="acc13", tag=f"bank{4 * (t - 2) + 2 * half + 1}")
                pass_w1(c, t, half, 1, start=True)
                pass_w1(c, t, half, 0)
                pass_w3(c, t, half, 0)
                pass_w3(c, t, half, 1, stop=True)
                join(t, half, c, acc23[t, half])
            row_max(t)

        HALF = M // 2
        faces01 = sbuf([P, 2, M], F32, "faces01", tag="bias_then_faces")
        faces23 = sbuf([P, 2, M], F32, "faces23")
        for t in range(PACK):
            nc.scalar.activation((faces01, faces23)[t // 2][:, t % 2, :], h[t][:].indirect(p2[:]), ACT.Sigmoid,
                                 bias=thr_c[:, t : t + 1])
        edges23 = sbuf([P, 2, M], F32, "edges23", tag="thr_then_edges")

        m_bf = sbuf([P, M * PACK], BF16, "m_bf")
        m_w = sbuf([P, M], U32, "m_w")
        m_sc = sbuf([P, M], U8, "m_sc")

        def weigh(pair, larger, lo, hi):
            dst = m_bf[:, lo * PACK : hi * PACK].rearrange("p (c i t) -> p c t i", i=4, t=PACK)
            nc.vector.tensor_tensor(
                dst[:, :, 2 * pair : 2 * pair + 2, :],
                larger[:].rearrange("p t (c i) -> p c t i", i=4),
                chair_sb[:, 2 * pair : 2 * pair + 2, lo:hi].rearrange("p t (c i) -> p c t i", i=4),
                ALU.mult)

        larger01 = sbuf([P, 2, M], F32, "larger01", tag="sum23_3_1")
        for t in range(2):
            nc.vector.scalar_tensor_tensor(larger01[:, t, :], faces01[:, t, :], lean_c[:, t : t + 1], edges01[:, t, :],
                                           ALU.add, ALU.max)
        weigh(0, larger01, 0, M)

        w4_bf = sbuf([P, N * PACK], BF16, "w4_bf")
        w4_sc = sbuf([P, N], U8, "w4_sc")
        w4_blocks = []
        lo = 0
        for g, blocks in enumerate(W4_BLOCKS):
            hi = lo + blocks * P
            w4_w = sbuf([P, hi - lo], U32, f"w4_w{g}", tag="sum23_3_1" if hi == N else "")
            for c0 in range(lo, hi, P):
                nc.gpsimd.tensor_scalar(
                    w4_bf[:, c0 * PACK : (c0 + P) * PACK].rearrange("p (n j) -> p n j", j=PACK),
                    w4_raw[:, :, c0 : c0 + P].rearrange("p j n -> p n j"), 1.0, 0.0, ALU.mult, ALU.add)
                w4_blocks.append(w4_w[:, c0 - lo : c0 - lo + P])
            nc.vector.quantize_mx(out=w4_w[:].bitcast(FP8X4), scales=w4_sc[:, lo:hi],
                                  in_=w4_bf[:, lo * PACK : hi * PACK])
            lo = hi

        out_v = out.rearrange("(g e p) m -> g p e m", e=2, p=P)
        for half in range(2):
            lo, hi = half * HALF, (half + 1) * HALF
            larger23 = sbuf([P, 2, HALF], F32, "larger23")
            for t in range(2, PACK):
                nc.scalar.activation(edges23[:, t - 2, lo:hi], h[t][:].indirect(p1[:, lo // 16 : hi // 16]), ACT.Exp,
                                     bias=bias_col(t), scale=temp_c[:, t : t + 1])
                nc.vector.scalar_tensor_tensor(larger23[:, t - 2, :], faces23[:, t - 2, lo:hi], lean_c[:, t : t + 1],
                                               edges23[:, t - 2, lo:hi], ALU.add, ALU.max)
            weigh(1, larger23, lo, hi)
            nc.vector.quantize_mx(out=m_w[:, lo:hi].bitcast(FP8X4), scales=m_sc[:, lo:hi],
                                  in_=m_bf[:, lo * PACK : hi * PACK])
        for half in range(2):
            lo, hi = half * HALF, (half + 1) * HALF
            for g in range(N // (2 * P)):
                step = half * (N // (2 * P)) + g
                z = psum.tile([P, 2, HALF], F32, name="z", tag=f"bank{2 * step % 8}")
                y = psum.tile([P, 2, HALF], F32, name="y", tag=f"bank{(2 * step + 1) % 8}")
                for e in range(2):
                    n_cols = rows(2 * g + e)
                    nc.tensor.matmul_mx(z[:, e, :], lhsT=w5_w[:, n_cols].bitcast(FP4X4), lhsT_scale=w5_sc[:, n_cols],
                                        rhs=m_w[:, lo:hi].bitcast(FP8X4), rhs_scale=m_sc[:, lo:hi],
                                        start=True, stop=True)
                for e in range(2):
                    n_cols = rows(2 * g + e)
                    nc.tensor.matmul_mx(y[:, e, :], lhsT=w4_blocks[2 * g + e].bitcast(FP8X4), lhsT_scale=w4_sc[:, n_cols],
                                        rhs=m_w[:, lo:hi].bitcast(FP8X4), rhs_scale=m_sc[:, lo:hi],
                                        start=True, stop=True)
                square = sbuf([P, 2, HALF], F32, f"square{half}_{g}")
                result = sbuf([P, 2, HALF], F32, f"result{half}_{g}")
                nc.scalar.activation(square[:], z[:], ACT.Square)
                pieces = (slice(0, 1), slice(1, 2)) if step == LAST_STEP else (slice(0, 2),)
                for piece in pieces:
                    nc.vector.tensor_tensor(result[:, piece], y[:, piece], square[:, piece], ALU.subtract)
                    nc.sync.dma_start(out=out_v[g][:, piece, lo:hi], in_=result[:, piece])
